import numpy as np
import ml_dtypes


def mxq(x, axis, fmt="e4m3"):
    dtype, down = {"e4m3": (ml_dtypes.float8_e4m3fn, 7), "e5m2": (ml_dtypes.float8_e5m2, 14)}[fmt]
    v = np.moveaxis(np.asarray(x, np.float32).astype(ml_dtypes.bfloat16).astype(np.float64), axis, -1)
    blocks = v.reshape(v.shape[:-1] + (-1, 32))
    amax = np.abs(blocks).max(-1, keepdims=True)
    byte = np.maximum(np.where(amax > 0, np.frexp(amax)[1] - 1 + 127, 0) - down, 1)
    scale = np.exp2(byte - 127.0)
    codes = (blocks / scale).astype(np.float32).astype(dtype).astype(np.float64)
    return np.moveaxis((codes * scale).reshape(v.shape), -1, axis)


WIDE = False


def mx_kscale(k):
    if not WIDE:
        return np.ones(k)
    levels = np.array([10, -10, 5, -5, 0])
    if k % 512:
        return np.exp2(np.random.permutation(np.resize(levels, k // 32))).repeat(32)
    a = np.empty((k // 512, 16))
    for p in range(k // 512):
        a[p, :8] = np.random.permutation(np.resize(levels, 8))
        for g in range(8):
            far = levels[np.abs(levels - a[p, g]) >= 10]
            a[p, g + 8] = far[np.random.randint(len(far))]
    return np.exp2(a.ravel()).repeat(32)


def f64(x):
    return np.asarray(x).astype(np.float64)


def striped(idx):
    return np.tile(idx.reshape(-1, 16).T, (8, 1)).astype(np.uint16)


def unstriped(offs):
    return offs[:16].T.reshape(-1).astype(np.int64)


def striped8(idx):
    return np.concatenate([x.reshape(-1, 16).T for x in idx]).astype(np.uint16)


def runs(offs, k):
    lists = np.stack([offs[16 * r : 16 * r + 16].T.reshape(-1) for r in range(8)]).astype(np.int64)
    return lists[np.arange(k) % 512 // 64]


def pack_weight(w):
    k, n = w.shape
    w = f64(np.asarray(w, np.float32).astype(ml_dtypes.bfloat16)).reshape(k // 32, 32, n)
    amax = np.abs(w).max(1)
    byte = np.clip(np.where(amax > 0, np.frexp(amax)[1] - 1 + 127 - 7, 1), 1, 254)
    scaled = (w * np.exp2(127.0 - byte)[:, None, :]).reshape(k, n).astype(np.float32)
    words = np.ascontiguousarray(scaled.reshape(k // 512, 128, 4, n).transpose(0, 1, 3, 2)).astype(ml_dtypes.float8_e4m3fn).view(np.uint8)
    return words, np.ascontiguousarray(byte.astype(np.uint8).reshape(k // 512, 16, n))


def unpack_weight(words, scales):
    g, p, n, _ = words.shape
    vals = np.ascontiguousarray(words).view(ml_dtypes.float8_e4m3fn).astype(np.float64) * np.repeat(np.exp2(scales.astype(np.float64) - 127.0), 8, axis=1)[..., None]
    return vals.transpose(0, 1, 3, 2).reshape(g * 512, n)


def relu(v):
    return np.maximum(v, 0.0)


K, T, S, V, N, H = 512, 2048, 512, 512, 512, 512


def setup_inputs():
    n = np.random.standard_normal
    s = mx_kscale(K)[:, None]
    u = mx_kscale(H)
    packed_xT = pack_weight(n((K, T)) * s)
    return {
        "x_words": packed_xT[0],
        "x_scales": packed_xT[1],
        "w1": (n((K, H)) / np.sqrt(K) / s * u).astype(np.float32),
        "a1": np.repeat(np.random.uniform(0.1, 0.5, (8, V)), 64, axis=0).astype(np.float32),
        "a2": np.repeat(np.random.uniform(0.1, 0.5, (8, V)), 64, axis=0).astype(np.float32),
        "a3": np.repeat(np.random.uniform(0.1, 0.5, (8, V)), 64, axis=0).astype(np.float32),
        "a4": np.repeat(np.random.uniform(0.1, 0.5, (8, V)), 64, axis=0).astype(np.float32),
        "w2": (n((H, H)) / np.sqrt(H) / u[:, None] * u).astype(np.float32),
        "res": (2 * n((N, V))).astype(np.float32),
        "w3": (n((H, N)) / np.sqrt(H) / u[:, None]).astype(np.float32),
        "offs": striped(np.random.permutation(T)[:S]),
        "c1": striped8(np.random.randint(0, S, (8, V))),
        "c2": striped8(np.random.randint(0, S, (8, V))),
        "c3": striped8(np.random.randint(0, S, (8, V))),
        "c4": striped8(np.random.randint(0, S, (8, V))),
    }


def reference(x_words, x_scales, w1, a1, a2, a3, a4, w2, res, w3, offs, c1, c2, c3, c4):
    xq = unpack_weight(x_words, x_scales)[:, unstriped(offs)]
    y = mxq(f64(w1), 0, "e4m3").T @ xq
    z = (y[np.arange(H)[:, None], runs(c1, H)]) * f64(a1) + (y[np.arange(H)[:, None], runs(c2, H)]) * f64(a2) + (y[np.arange(H)[:, None], runs(c3, H)]) * f64(a3) + (y[np.arange(H)[:, None], runs(c4, H)]) * f64(a4)
    h = relu(mxq(f64(w2), 0, "e4m3").T @ mxq(z, 0, "e4m3"))
    return f64(res) + (mxq(f64(w3), 0, "e4m3").T @ mxq(h, 0, "e4m3"))

@@ -1,0 +1,190 @@
+from contextlib import ExitStack
+
+import concourse.mybir as mybir
+from concourse.masks import make_identity
+
+K, T, S, V, N, H = 512, 2048, 512, 512, 512, 512
+FLOPS = 3 * 2 * 512 * 512 * 512
+BYTES = K * T + 16 * T + 5 * 4 * 512 * 512 + 4 * 8 * V * 4 + 5 * 128 * 32 * 2
+
+F32 = mybir.dt.float32
+BF16 = mybir.dt.bfloat16
+I32 = mybir.dt.int32
+U32 = mybir.dt.uint32
+U16 = mybir.dt.uint16
+U8 = mybir.dt.uint8
+FP8X4 = mybir.dt.float8_e4m3fn_x4
+MULT = mybir.AluOpType.mult
+ADD = mybir.AluOpType.add
+RELU = mybir.ActivationFunctionType.Relu
+
+P = 128
+PACK = 4
+LANES = 16
+CHUNKS = ((0, 256), (256, 128), (384, 128))
+
+
+def tile_picked_hgrid_relu_p_kernel(
+    tc, x_words, x_scales, w1, a1, a2, a3, a4, w2, res, w3, offs, c1, c2, c3, c4, out
+):
+    nc = tc.nc
+    with ExitStack() as ctx:
+        lists = ctx.enter_context(tc.tile_pool(name="lists", bufs=1))
+        keep = ctx.enter_context(tc.tile_pool(name="keep", bufs=1))
+        ring = ctx.enter_context(tc.tile_pool(name="ring", bufs=2))
+        psum = ctx.enter_context(tc.psum_pool(name="psum", bufs=1))
+
+        def load_list(dram, name):
+            tile = lists.tile([P, S // LANES], U16, name=name)
+            nc.sync.dma_start(tile[:], dram)
+            return tile
+
+        def load_weight(dram, name):
+            raw = keep.tile([P, PACK, H], F32, name=name)
+            nc.sync.dma_start(raw[:], dram.rearrange("(p j) c -> p j c", j=PACK))
+            return raw
+
+        def mx(out_ap, w_codes, w_scales, cols, codes, scales):
+            nc.tensor.matmul_mx(
+                out=out_ap, lhsT=w_codes[:, cols].bitcast(FP8X4), lhsT_scale=w_scales[:, cols],
+                rhs=codes.bitcast(FP8X4), rhs_scale=scales, start=True, stop=True,
+            )
+
+        def quantize(codes, scales, grouped):
+            nc.vector.quantize_mx(out=codes.bitcast(FP8X4), scales=scales, in_=grouped)
+
+        picked = load_list(offs, "picked")
+        w1_raw = load_weight(w1, "w1_raw")
+        table_scales = keep.tile([P, T], U8, name="table_scales")
+        nc.vector.memset(table_scales[:].bitcast(I32), 0)
+        for q in range(4):
+            nc.scalar.dma_start(
+                table_scales[32 * q : 32 * q + 4, :].bitcast(I32),
+                x_scales[0, 4 * q : 4 * q + 4, :].bitcast(I32),
+            )
+        table_words = keep.tile([P, T], I32, name="table_words")
+        nc.sync.dma_start(table_words[:], x_words[0].rearrange("p n t -> p (n t)").bitcast(I32))
+        corners = []
+        gains = []
+        for c, (c_dram, a_dram) in enumerate(((c1, a1), (c2, a2), (c3, a3), (c4, a4))):
+            corners.append(load_list(c_dram, "corner%d" % c))
+            gain = keep.tile([P, V], F32, name="gain%d" % c)
+            nc.sync.dma_start(gain[:], a_dram.rearrange("(p j) v -> p j v", j=PACK)[:, 0, :])
+            gains.append(gain)
+        w2_raw = load_weight(w2, "w2_raw")
+        w3_raw = load_weight(w3, "w3_raw")
+        res_sb = keep.tile([P, PACK, V], F32, name="res_sb")
+        nc.sync.dma_start(res_sb[:], res.rearrange("(t p) v -> p t v", p=P))
+
+        ident = keep.tile([P, P], F32, name="ident")
+        make_identity(nc, ident[:])
+
+        def dealt_cast(copy, raw, t0, name):
+            grouped = keep.tile([P, 2 * P * PACK], BF16, name=name, align_bytes=64)
+            copy(
+                out=grouped[:].rearrange("p (t m j) -> p m t j", t=2, j=PACK),
+                in_=raw[:].rearrange("p j (m t) -> p m t j", t=PACK)[:, :, t0 : t0 + 2, :],
+            )
+            return grouped
+
+        def planes(name, width):
+            codes = keep.tile([P, width], U32, name=name + "_codes", align_bytes=64)
+            scales = keep.tile([P, width], U8, name=name + "_scales", align_bytes=64)
+            return codes, scales
+
+        w1_codes, w1_scales = planes("w1", H)
+        w1_lo = dealt_cast(nc.vector.tensor_copy, w1_raw, 0, "w1_lo")
+        w1_hi = dealt_cast(nc.scalar.copy, w1_raw, 2, "w1_hi")
+        x_codes, x_bytes = planes("x", S)
+        nc.vector.tensor_copy(x_bytes[:], table_scales[:].indirect(picked[:]))
+        quantize(w1_codes[:, 0:256], w1_scales[:, 0:256], w1_lo[:])
+        quantize(w1_codes[:, 256:512], w1_scales[:, 256:512], w1_hi[:])
+
+        half = S // 2
+        y = [keep.tile([P, S], F32, name="y%d" % t) for t in range(PACK)]
+        y0_banks = [psum.tile([P, S], F32, name="y0_bank%d" % u, tag="wide", bufs=4) for u in range(2)]
+        y_banks = [psum.tile([P, S], F32, name="y_bank1", tag="wide", bufs=4),
+                   psum.tile([P, S], F32, name="y_bank2", tag="wide", bufs=4),
+                   psum.tile([P, S], F32, name="y_bank3", tag="hidden", bufs=2)]
+        for u in range(2):
+            cols = slice(u * half, (u + 1) * half)
+            nc.vector.tensor_copy(
+                x_codes[:, cols],
+                table_words[:].bitcast(U32).indirect(picked[:, u * half // LANES : (u + 1) * half // LANES]),
+            )
+            mx(y0_banks[u][:, 0:half], w1_codes, w1_scales, slice(0, P), x_codes[:, cols], x_bytes[:, cols])
+            for t in range(1, PACK):
+                mx(y_banks[t - 1][:, cols], w1_codes, w1_scales, slice(t * P, (t + 1) * P), x_codes[:, cols], x_bytes[:, cols])
+        nc.scalar.copy(y[0][:, 0:half], y0_banks[0][:, 0:half])
+        nc.vector.tensor_copy(y[0][:, half:S], y0_banks[1][:, 0:half])
+        for t in range(1, PACK):
+            nc.scalar.copy(y[t][:], y_banks[t - 1][:])
+
+        w2_codes, w2_scales = planes("w2", H)
+        for u in range(2):
+            grouped = dealt_cast(nc.scalar.copy, w2_raw, 2 * u, "w2_half%d" % u)
+            quantize(w2_codes[:, 256 * u : 256 * (u + 1)], w2_scales[:, 256 * u : 256 * (u + 1)], grouped[:])
+        w3_codes, w3_scales = planes("w3", N)
+        w3_grouped = keep.tile([P, N, PACK], BF16, name="w3_grouped", align_bytes=64)
+        nc.scalar.copy(out=w3_grouped[:], in_=w3_raw[:].rearrange("p j c -> p c j"))
+        quantize(w3_codes[:], w3_scales[:], w3_grouped[:].rearrange("p c j -> p (c j)"))
+
+        out_view = out.rearrange("(t p) v -> p t v", p=P)
+
+        def finish(v0, sums):
+            turned = ring.tile([P, 2, P, 2], BF16, name="turned")
+            nc.scalar.copy(out=turned[:], in_=sums[:].rearrange("v (u e p) -> v u p e", u=2, e=2))
+            words = turned[:].rearrange("v u p e -> v (u p e)").bitcast(F32)
+            back = psum.tile([P, 2 * P], F32, name="back", tag="back", bufs=1)
+            for u in range(2):
+                nc.tensor.transpose(back[:, u * P : (u + 1) * P], words[:, u * P : (u + 1) * P], ident[:])
+            z_grouped = ring.tile([P, P * PACK], BF16, name="z_grouped", align_bytes=64)
+            nc.scalar.copy(
+                out=z_grouped[:].bitcast(F32).rearrange("p (v u) -> p v u", u=2),
+                in_=back[:].rearrange("p (u v) -> p v u", u=2),
+            )
+            z_codes = ring.tile([P, P], U32, name="z_codes", align_bytes=64)
+            z_scales = ring.tile([P, P], U8, name="z_scales", align_bytes=64)
+            quantize(z_codes[:], z_scales[:], z_grouped[:])
+            hidden = psum.tile([P, H], F32, name="hidden", tag="hidden", bufs=2)
+            for t in range(PACK):
+                cols = slice(t * P, (t + 1) * P)
+                mx(hidden[:, cols], w2_codes, w2_scales, cols, z_codes[:], z_scales[:])
+            h_grouped = ring.tile([P, P * PACK], BF16, name="h_grouped", align_bytes=64)
+            nc.scalar.activation(
+                out=h_grouped[:].rearrange("p (v t) -> p v t", t=PACK),
+                in_=hidden[:].rearrange("p (t v) -> p v t", t=PACK),
+                func=RELU,
+            )
+            h_codes = ring.tile([P, P], U32, name="h_codes", align_bytes=64)
+            h_scales = ring.tile([P, P], U8, name="h_scales", align_bytes=64)
+            quantize(h_codes[:], h_scales[:], h_grouped[:])
+            last = psum.tile([P, N], F32, name="last", tag="last", bufs=1)
+            for t in range(PACK):
+                cols = slice(t * P, (t + 1) * P)
+                mx(last[:, cols], w3_codes, w3_scales, cols, h_codes[:], h_scales[:])
+            result = ring.tile([P, PACK, P], F32, name="result")
+            nc.vector.tensor_tensor(
+                result[:], last[:].rearrange("p (t v) -> p t v", t=PACK), res_sb[:, :, v0 : v0 + P], ADD
+            )
+            nc.sync.dma_start(out_view[:, :, v0 : v0 + P], result[:])
+
+        for v0, n in CHUNKS:
+            blocks = n // P
+            sums = [psum.tile([P, H], F32, name="sums%d" % b, tag="wide", bufs=4) for b in range(blocks)]
+            for t in range(PACK):
+                for c in range(4):
+                    term = ring.tile([P, n], F32, name="term", bufs=8)
+                    nc.vector.tensor_tensor(
+                        term[:],
+                        y[t][:].indirect(corners[c][:, v0 // LANES : (v0 + n) // LANES]),
+                        gains[c][:, v0 : v0 + n],
+                        MULT,
+                    )
+                    for b in range(blocks):
+                        nc.tensor.matmul(
+                            sums[b][:, t * P : (t + 1) * P], lhsT=term[:, b * P : (b + 1) * P], rhs=ident[:],
+                            is_transpose=True, start=(c == 0), stop=(c == 3),
+                        )
+            for b in range(blocks):
+                finish(v0 + b * P, sums[b])

@@ -21,7 +21,6 @@ RELU = mybir.ActivationFunctionType.Relu
 P = 128
 PACK = 4
 LANES = 16
-CHUNKS = ((0, 256), (256, 128), (384, 128))
 
 
 def tile_picked_hgrid_relu_p_kernel(
@@ -31,7 +30,6 @@ def tile_picked_hgrid_relu_p_kernel(
     with ExitStack() as ctx:
         lists = ctx.enter_context(tc.tile_pool(name="lists", bufs=1))
         keep = ctx.enter_context(tc.tile_pool(name="keep", bufs=1))
-        ring = ctx.enter_context(tc.tile_pool(name="ring", bufs=2))
         psum = ctx.enter_context(tc.psum_pool(name="psum", bufs=1))
 
         def load_list(dram, name):
@@ -40,7 +38,7 @@ def tile_picked_hgrid_relu_p_kernel(
             return tile
 
         def load_weight(dram, name):
-            raw = keep.tile([P, PACK, H], F32, name=name)
+            raw = keep.tile([P, PACK, H], F32, name=name, tag=name, align_bytes=64)
             nc.sync.dma_start(raw[:], dram.rearrange("(p j) c -> p j c", j=PACK))
             return raw
 
@@ -53,25 +51,32 @@ def tile_picked_hgrid_relu_p_kernel(
         def quantize(codes, scales, grouped):
             nc.vector.quantize_mx(out=codes.bitcast(FP8X4), scales=scales, in_=grouped)
 
-        picked = load_list(offs, "picked")
         w1_raw = load_weight(w1, "w1_raw")
+        picked = load_list(offs, "picked")
         table_scales = keep.tile([P, T], U8, name="table_scales")
-        nc.vector.memset(table_scales[:].bitcast(I32), 0)
+        nc.gpsimd.memset(table_scales[:].bitcast(I32), 0)
         for q in range(4):
-            nc.scalar.dma_start(
+            nc.sync.dma_start(
                 table_scales[32 * q : 32 * q + 4, :].bitcast(I32),
                 x_scales[0, 4 * q : 4 * q + 4, :].bitcast(I32),
             )
         table_words = keep.tile([P, T], I32, name="table_words")
         nc.sync.dma_start(table_words[:], x_words[0].rearrange("p n t -> p (n t)").bitcast(I32))
-        corners = []
-        gains = []
-        for c, (c_dram, a_dram) in enumerate(((c1, a1), (c2, a2), (c3, a3), (c4, a4))):
-            corners.append(load_list(c_dram, "corner%d" % c))
-            gain = keep.tile([P, V], F32, name="gain%d" % c)
-            nc.sync.dma_start(gain[:], a_dram.rearrange("(p j) v -> p j v", j=PACK)[:, 0, :])
-            gains.append(gain)
+
+        def load_gain(dram, name):
+            gain = keep.tile([P, V], F32, name=name)
+            nc.sync.dma_start(gain[:], dram.rearrange("(p j) v -> p j v", j=PACK)[:, 0, :])
+            return gain
+
+        corners = [load_list(c1, "corner0")]
+        gains = [load_gain(a1, "gain0")]
+        corners.append(load_list(c2, "corner1"))
+        gains.append(load_gain(a2, "gain1"))
+        corners.append(load_list(c3, "corner2"))
+        corners.append(load_list(c4, "corner3"))
         w2_raw = load_weight(w2, "w2_raw")
+        gains.append(load_gain(a3, "gain2"))
+        gains.append(load_gain(a4, "gain3"))
         w3_raw = load_weight(w3, "w3_raw")
         res_sb = keep.tile([P, PACK, V], F32, name="res_sb")
         nc.sync.dma_start(res_sb[:], res.rearrange("(t p) v -> p t v", p=P))
@@ -101,11 +106,13 @@ def tile_picked_hgrid_relu_p_kernel(
         quantize(w1_codes[:, 256:512], w1_scales[:, 256:512], w1_hi[:])
 
         half = S // 2
-        y = [keep.tile([P, S], F32, name="y%d" % t) for t in range(PACK)]
+        y = [keep.tile([P, 2 * S if t < 2 else S], F32, name="y%d" % t) for t in range(PACK)]
+        for t in range(2):
+            nc.gpsimd.memset(y[t][:, S : 2 * S], 0.0)
         y0_banks = [psum.tile([P, S], F32, name="y0_bank%d" % u, tag="wide", bufs=4) for u in range(2)]
         y_banks = [psum.tile([P, S], F32, name="y_bank1", tag="wide", bufs=4),
-                   psum.tile([P, S], F32, name="y_bank2", tag="wide", bufs=4),
-                   psum.tile([P, S], F32, name="y_bank3", tag="hidden", bufs=2)]
+                   psum.tile([P, S], F32, name="y_bank2", tag="last", bufs=2),
+                   psum.tile([P, S], F32, name="y_bank3", tag="last", bufs=2)]
         for u in range(2):
             cols = slice(u * half, (u + 1) * half)
             nc.vector.tensor_copy(
@@ -118,7 +125,7 @@ def tile_picked_hgrid_relu_p_kernel(
         nc.scalar.copy(y[0][:, 0:half], y0_banks[0][:, 0:half])
         nc.vector.tensor_copy(y[0][:, half:S], y0_banks[1][:, 0:half])
         for t in range(1, PACK):
-            nc.scalar.copy(y[t][:], y_banks[t - 1][:])
+            nc.scalar.copy(y[t][:, 0:S], y_banks[t - 1][:])
 
         w2_codes, w2_scales = planes("w2", H)
         for u in range(2):
@@ -131,60 +138,147 @@ def tile_picked_hgrid_relu_p_kernel(
 
         out_view = out.rearrange("(t p) v -> p t v", p=P)
 
-        def finish(v0, sums):
-            turned = ring.tile([P, 2, P, 2], BF16, name="turned")
-            nc.scalar.copy(out=turned[:], in_=sums[:].rearrange("v (u e p) -> v u p e", u=2, e=2))
-            words = turned[:].rearrange("v u p e -> v (u p e)").bitcast(F32)
-            back = psum.tile([P, 2 * P], F32, name="back", tag="back", bufs=1)
-            for u in range(2):
-                nc.tensor.transpose(back[:, u * P : (u + 1) * P], words[:, u * P : (u + 1) * P], ident[:])
-            z_grouped = ring.tile([P, P * PACK], BF16, name="z_grouped", align_bytes=64)
-            nc.scalar.copy(
-                out=z_grouped[:].bitcast(F32).rearrange("p (v u) -> p v u", u=2),
-                in_=back[:].rearrange("p (u v) -> p v u", u=2),
+        def work(shape, dtype, name, tag=None):
+            return keep.tile(shape, dtype, name=name, tag=tag or name, align_bytes=64)
+
+        def gather(term, t, c, v0, n):
+            nc.vector.tensor_tensor(
+                term,
+                y[t][:].indirect(corners[c][:, v0 // LANES : (v0 + n) // LANES]),
+                gains[c][:, v0 : v0 + n],
+                MULT,
             )
-            z_codes = ring.tile([P, P], U32, name="z_codes", align_bytes=64)
-            z_scales = ring.tile([P, P], U8, name="z_scales", align_bytes=64)
+
+        def add_turned(term, c, banks, place):
+            for b, bank in enumerate(banks):
+                nc.tensor.matmul(
+                    bank[:, place * P : (place + 1) * P], lhsT=term[:, b * P : (b + 1) * P], rhs=ident[:],
+                    is_transpose=True, start=(c == 0), stop=(c == 3),
+                )
+
+        def round_pair(turned, u, bank):
+            nc.scalar.copy(out=turned[:, u], in_=bank[:, 0 : 2 * P].rearrange("v (e p) -> v p e", e=2))
+
+        def turn_back(b, pairs):
+            words = turned[b][:].rearrange("v u p e -> v (u p e)").bitcast(F32)
+            back = psum.tile([P, 2 * P], F32, name="back", tag="back", bufs=1)
+            for u in range(pairs):
+                nc.tensor.transpose(back[:, u * P : (u + 1) * P], words[:, u * P : (u + 1) * P], ident[:])
+            z_grouped = work([P, P * PACK], BF16, "z_grouped%d" % b)
+            nc.scalar.copy(
+                out=z_grouped[:].bitcast(F32).rearrange("p (v u) -> p v u", u=2)[:, :, 0:pairs],
+                in_=back[:].rearrange("p (u v) -> p v u", u=2)[:, :, 0:pairs],
+            )
+            return z_grouped
+
+        def network(b, z_grouped, banks):
+            z_codes = work([P, P], U32, "z_codes%d" % b)
+            z_scales = work([P, P], U8, "z_scales%d" % b)
             quantize(z_codes[:], z_scales[:], z_grouped[:])
-            hidden = psum.tile([P, H], F32, name="hidden", tag="hidden", bufs=2)
+            hidden = psum.tile([P, H], F32, name="hidden", tag="hidden", bufs=1)
             for t in range(PACK):
                 cols = slice(t * P, (t + 1) * P)
                 mx(hidden[:, cols], w2_codes, w2_scales, cols, z_codes[:], z_scales[:])
-            h_grouped = ring.tile([P, P * PACK], BF16, name="h_grouped", align_bytes=64)
+            h_grouped = work([P, P * PACK], BF16, "h_grouped%d" % b)
             nc.scalar.activation(
                 out=h_grouped[:].rearrange("p (v t) -> p v t", t=PACK),
                 in_=hidden[:].rearrange("p (t v) -> p v t", t=PACK),
                 func=RELU,
             )
-            h_codes = ring.tile([P, P], U32, name="h_codes", align_bytes=64)
-            h_scales = ring.tile([P, P], U8, name="h_scales", align_bytes=64)
+            h_codes = work([P, P], U32, "h_codes%d" % b)
+            h_scales = work([P, P], U8, "h_scales%d" % b)
             quantize(h_codes[:], h_scales[:], h_grouped[:])
-            last = psum.tile([P, N], F32, name="last", tag="last", bufs=1)
+            per_bank = PACK // len(banks)
             for t in range(PACK):
-                cols = slice(t * P, (t + 1) * P)
-                mx(last[:, cols], w3_codes, w3_scales, cols, h_codes[:], h_scales[:])
-            result = ring.tile([P, PACK, P], F32, name="result")
-            nc.vector.tensor_tensor(
-                result[:], last[:].rearrange("p (t v) -> p t v", t=PACK), res_sb[:, :, v0 : v0 + P], ADD
-            )
-            nc.sync.dma_start(out_view[:, :, v0 : v0 + P], result[:])
+                bank = banks[t // per_bank]
+                place = t % per_bank
+                mx(bank[:, place * P : (place + 1) * P], w3_codes, w3_scales, slice(t * P, (t + 1) * P), h_codes[:], h_scales[:])
 
-        for v0, n in CHUNKS:
-            blocks = n // P
-            sums = [psum.tile([P, H], F32, name="sums%d" % b, tag="wide", bufs=4) for b in range(blocks)]
-            for t in range(PACK):
-                for c in range(4):
-                    term = ring.tile([P, n], F32, name="term", bufs=8)
-                    nc.vector.tensor_tensor(
-                        term[:],
-                        y[t][:].indirect(corners[c][:, v0 // LANES : (v0 + n) // LANES]),
-                        gains[c][:, v0 : v0 + n],
-                        MULT,
-                    )
-                    for b in range(blocks):
-                        nc.tensor.matmul(
-                            sums[b][:, t * P : (t + 1) * P], lhsT=term[:, b * P : (b + 1) * P], rhs=ident[:],
-                            is_transpose=True, start=(c == 0), stop=(c == 3),
-                        )
-            for b in range(blocks):
-                finish(v0 + b * P, sums[b])
+        def leave(queue, result, bank, t0, tiles, v0):
+            nc.vector.tensor_tensor(
+                result,
+                bank[:, 0 : tiles * P].rearrange("p (t v) -> p t v", t=tiles),
+                res_sb[:, t0 : t0 + tiles, v0 : v0 + P],
+                ADD,
+            )
+            queue.dma_start(out_view[:, t0 : t0 + tiles, v0 : v0 + P], result)
+
+        def wide_bank(name):
+            return psum.tile([P, H], F32, name=name, tag="wide", bufs=4)
+
+        def last_bank(b):
+            return psum.tile([P, N], F32, name="last%d" % b, tag="last", bufs=2)
+
+        turned = [work([P, 2 if b < 3 else 1, P, 2], BF16, "turned%d" % b) for b in range(4)]
+
+        sums = [wide_bank("low%d" % b) for b in range(4)]
+        first = work([P, 7, V], F32, "terms_first")
+        second = work([P, V + 8 * 2 * P + 6 * P], F32, "terms_second", "w3_raw")
+        for t in range(2):
+            for c in range(4):
+                term = first[:, 4 * t + c, :] if 4 * t + c < 7 else second[:, 0:V]
+                gather(term, t, c, 0, V)
+                add_turned(term, c, sums, t)
+        for b in range(4):
+            round_pair(turned[b], 0, sums[b])
+        z_last = turn_back(3, 1)
+
+        sums = [wide_bank("high%d" % b) for b in range(2)]
+        for e in range(2):
+            for c in range(4):
+                at = V + (4 * e + c) * 2 * P
+                gather(second[:, at : at + 2 * P], 2 + e, c, 0, 2 * P)
+                add_turned(second[:, at : at + 2 * P], c, sums, e)
+        lasts = []
+        for b in range(2):
+            round_pair(turned[b], 1, sums[b])
+        for b in range(2):
+            lasts.append(last_bank(b))
+            network(b, turn_back(b, 2), [lasts[b]])
+
+        sums = [wide_bank("high2")]
+        third = work([P, 8 - 6 + 2 * 1, P], F32, "terms_third", "turned1")
+        for e in range(2):
+            for c in range(4):
+                g = 4 * e + c
+                at = V + 8 * 2 * P + g * P
+                term = second[:, at : at + P] if g < 6 else third[:, g - 6, :]
+                gather(term, 2 + e, c, 2 * P, P)
+                add_turned(term, c, sums, e)
+        round_pair(turned[2], 1, sums[0])
+        lasts.append(wide_bank("last2"))
+        network(2, turn_back(2, 2), [lasts[2]])
+
+        v0 = 3 * P
+        fourth = work([P, 2 * (3 - 1), P], F32, "terms_fourth", "z_codes0")
+        fifth = work([P, 2 * (4 - 3), P], F32, "terms_fifth", "z_codes1")
+        pairs = []
+        for c in range(4):
+            if c < 1:
+                pairs.append(third[:, 8 - 6 + 2 * c : 8 - 6 + 2 * c + 2, :])
+            elif c < 3:
+                pairs.append(fourth[:, 2 * (c - 1) : 2 * (c - 1) + 2, :])
+            else:
+                pairs.append(fifth[:, 2 * (c - 3) : 2 * (c - 3) + 2, :])
+            for e in range(2):
+                gather(pairs[c][:, e, :], 2 + e, c, v0, P)
+        partial = [work([P, 2, P], F32, "partial%d" % i) for i in range(2)]
+        nc.vector.tensor_tensor(partial[0][:], pairs[0], pairs[1], ADD)
+        nc.vector.tensor_tensor(partial[1][:], partial[0][:], pairs[2], ADD)
+        nc.vector.tensor_tensor(
+            z_last[:].rearrange("p (v t) -> p v t", t=PACK)[:, :, 2:4],
+            partial[1][:].rearrange("p e v -> p v e"),
+            pairs[3].rearrange("p e v -> p v e"),
+            ADD,
+        )
+        halves = [psum.tile([P, 2 * P], F32, name="last3_%d" % u, tag="wide", bufs=4) for u in range(2)]
+        network(3, z_last, halves)
+
+        early = work([P, 2, PACK, P], F32, "early", "z_grouped3")
+        for b in range(2):
+            leave(nc.sync, early[:, b], lasts[b], 0, PACK, b * P)
+        late = work([P, PACK, P], F32, "late", "h_grouped3")
+        leave(nc.sync, late[:], lasts[2], 0, PACK, 2 * P)
+        for u, queue in enumerate((nc.sync, nc.scalar)):
+            result = work([P, 2, P], F32, "result%d" % u)
+            leave(queue, result[:], halves[u], 2 * u, 2, v0)

@@ -84,11 +84,11 @@ def tile_picked_hgrid_relu_p_kernel(
         ident = keep.tile([P, P], F32, name="ident")
         make_identity(nc, ident[:])
 
-        def dealt_cast(copy, raw, t0, name):
-            grouped = keep.tile([P, 2 * P * PACK], BF16, name=name, align_bytes=64)
+        def dealt_cast(copy, raw, t0, name, count=2):
+            grouped = keep.tile([P, count * P * PACK], BF16, name=name, align_bytes=64)
             copy(
-                out=grouped[:].rearrange("p (t m j) -> p m t j", t=2, j=PACK),
-                in_=raw[:].rearrange("p j (m t) -> p m t j", t=PACK)[:, :, t0 : t0 + 2, :],
+                out=grouped[:].rearrange("p (t m j) -> p m t j", t=count, j=PACK),
+                in_=raw[:].rearrange("p j (m t) -> p m t j", t=PACK)[:, :, t0 : t0 + count, :],
             )
             return grouped
 
@@ -98,17 +98,16 @@ def tile_picked_hgrid_relu_p_kernel(
             return codes, scales
 
         w1_codes, w1_scales = planes("w1", H)
-        w1_lo = dealt_cast(nc.vector.tensor_copy, w1_raw, 0, "w1_lo")
-        w1_hi = dealt_cast(nc.scalar.copy, w1_raw, 2, "w1_hi")
+        w1_lo = dealt_cast(nc.vector.tensor_copy, w1_raw, 0, "w1_lo", 1)
+        w1_hi = dealt_cast(nc.scalar.copy, w1_raw, 1, "w1_hi", 3)
         x_codes, x_bytes = planes("x", S)
         nc.vector.tensor_copy(x_bytes[:], table_scales[:].indirect(picked[:]))
-        quantize(w1_codes[:, 0:256], w1_scales[:, 0:256], w1_lo[:])
-        quantize(w1_codes[:, 256:512], w1_scales[:, 256:512], w1_hi[:])
+        quantize(w1_codes[:, 0:128], w1_scales[:, 0:128], w1_lo[:])
 
         half = S // 2
         y = [keep.tile([P, 2 * S if t < 2 else S], F32, name="y%d" % t) for t in range(PACK)]
         for t in range(2):
-            nc.gpsimd.memset(y[t][:, S : 2 * S], 0.0)
+            nc.vector.memset(y[t][:, S : 2 * S], 0.0)
         y0_banks = [psum.tile([P, S], F32, name="y0_bank%d" % u, tag="wide", bufs=4) for u in range(2)]
         y_banks = [psum.tile([P, S], F32, name="y_bank1", tag="wide", bufs=4),
                    psum.tile([P, S], F32, name="y_bank2", tag="last", bufs=2),
@@ -120,8 +119,10 @@ def tile_picked_hgrid_relu_p_kernel(
                 table_words[:].bitcast(U32).indirect(picked[:, u * half // LANES : (u + 1) * half // LANES]),
             )
             mx(y0_banks[u][:, 0:half], w1_codes, w1_scales, slice(0, P), x_codes[:, cols], x_bytes[:, cols])
-            for t in range(1, PACK):
-                mx(y_banks[t - 1][:, cols], w1_codes, w1_scales, slice(t * P, (t + 1) * P), x_codes[:, cols], x_bytes[:, cols])
+        quantize(w1_codes[:, 128:256], w1_scales[:, 128:256], w1_hi[:, 0:512])
+        quantize(w1_codes[:, 256:512], w1_scales[:, 256:512], w1_hi[:, 512:1536])
+        for t in range(1, PACK):
+            mx(y_banks[t - 1][:], w1_codes, w1_scales, slice(t * P, (t + 1) * P), x_codes[:], x_bytes[:])
         nc.scalar.copy(y[0][:, 0:half], y0_banks[0][:, 0:half])
         nc.vector.tensor_copy(y[0][:, half:S], y0_banks[1][:, 0:half])
         for t in range(1, PACK):
@@ -156,18 +157,18 @@ def tile_picked_hgrid_relu_p_kernel(
                     is_transpose=True, start=(c == 0), stop=(c == 3),
                 )
 
-        def round_pair(turned, u, bank):
-            nc.scalar.copy(out=turned[:, u], in_=bank[:, 0 : 2 * P].rearrange("v (e p) -> v p e", e=2))
+        def round_pair(pair, bank):
+            nc.scalar.copy(out=pair, in_=bank[:, 0 : 2 * P].rearrange("v (e p) -> v p e", e=2))
 
         def turn_back(b, pairs):
-            words = turned[b][:].rearrange("v u p e -> v (u p e)").bitcast(F32)
-            back = psum.tile([P, 2 * P], F32, name="back", tag="back", bufs=1)
-            for u in range(pairs):
-                nc.tensor.transpose(back[:, u * P : (u + 1) * P], words[:, u * P : (u + 1) * P], ident[:])
+            back = wide_bank("back1") if b == 1 else psum.tile([P, H], F32, name="back", tag="back", bufs=1)
+            for u, pair in enumerate([low[:, b], high[b][:]][:pairs] if pairs == 2 else [low[:, b]]):
+                words = pair.rearrange("v p e -> v (p e)").bitcast(F32)
+                nc.tensor.transpose(back[:, u * P : (u + 1) * P], words, ident[:])
             z_grouped = work([P, P * PACK], BF16, "z_grouped%d" % b)
             nc.scalar.copy(
                 out=z_grouped[:].bitcast(F32).rearrange("p (v u) -> p v u", u=2)[:, :, 0:pairs],
-                in_=back[:].rearrange("p (u v) -> p v u", u=2)[:, :, 0:pairs],
+                in_=back[:, 0 : 2 * P].rearrange("p (u v) -> p v u", u=2)[:, :, 0:pairs],
             )
             return z_grouped
 
@@ -209,18 +210,19 @@ def tile_picked_hgrid_relu_p_kernel(
         def last_bank(b):
             return psum.tile([P, N], F32, name="last%d" % b, tag="last", bufs=2)
 
-        turned = [work([P, 2 if b < 3 else 1, P, 2], BF16, "turned%d" % b) for b in range(4)]
+        low = work([P, 4, P, 2], BF16, "low", "w3_raw")
+        high = [work([P, P, 2], BF16, "high%d" % b) for b in range(3)]
 
         sums = [wide_bank("low%d" % b) for b in range(4)]
         first = work([P, 7, V], F32, "terms_first")
-        second = work([P, V + 8 * 2 * P + 6 * P], F32, "terms_second", "w3_raw")
+        second = work([P, V + 8 * 2 * P + 7 * P], F32, "terms_second", "w2_raw")
         for t in range(2):
             for c in range(4):
                 term = first[:, 4 * t + c, :] if 4 * t + c < 7 else second[:, 0:V]
                 gather(term, t, c, 0, V)
                 add_turned(term, c, sums, t)
         for b in range(4):
-            round_pair(turned[b], 0, sums[b])
+            round_pair(low[:, b], sums[b])
         z_last = turn_back(3, 1)
 
         sums = [wide_bank("high%d" % b) for b in range(2)]
@@ -231,33 +233,33 @@ def tile_picked_hgrid_relu_p_kernel(
                 add_turned(second[:, at : at + 2 * P], c, sums, e)
         lasts = []
         for b in range(2):
-            round_pair(turned[b], 1, sums[b])
+            round_pair(high[b][:], sums[b])
         for b in range(2):
             lasts.append(last_bank(b))
             network(b, turn_back(b, 2), [lasts[b]])
 
         sums = [wide_bank("high2")]
-        third = work([P, 8 - 6 + 2 * 1, P], F32, "terms_third", "turned1")
+        third = work([P, 8 - 7 + 2 * 2, P], F32, "terms_third", "high1")
         for e in range(2):
             for c in range(4):
                 g = 4 * e + c
                 at = V + 8 * 2 * P + g * P
-                term = second[:, at : at + P] if g < 6 else third[:, g - 6, :]
+                term = second[:, at : at + P] if g < 7 else third[:, g - 7, :]
                 gather(term, 2 + e, c, 2 * P, P)
                 add_turned(term, c, sums, e)
-        round_pair(turned[2], 1, sums[0])
+        round_pair(high[2][:], sums[0])
         lasts.append(wide_bank("last2"))
         network(2, turn_back(2, 2), [lasts[2]])
 
         v0 = 3 * P
-        fourth = work([P, 2 * (3 - 1), P], F32, "terms_fourth", "z_codes0")
+        fourth = work([P, 2 * (3 - 2), P], F32, "terms_fourth", "z_codes0")
         fifth = work([P, 2 * (4 - 3), P], F32, "terms_fifth", "z_codes1")
         pairs = []
         for c in range(4):
-            if c < 1:
-                pairs.append(third[:, 8 - 6 + 2 * c : 8 - 6 + 2 * c + 2, :])
+            if c < 2:
+                pairs.append(third[:, 8 - 7 + 2 * c : 8 - 7 + 2 * c + 2, :])
             elif c < 3:
-                pairs.append(fourth[:, 2 * (c - 1) : 2 * (c - 1) + 2, :])
+                pairs.append(fourth[:, 2 * (c - 2) : 2 * (c - 2) + 2, :])
             else:
                 pairs.append(fifth[:, 2 * (c - 3) : 2 * (c - 3) + 2, :])
             for e in range(2):

from contextlib import ExitStack

import concourse.mybir as mybir
from concourse.masks import make_identity

K, T, S, V, N, H = 512, 2048, 512, 512, 512, 512
FLOPS = 3 * 2 * 512 * 512 * 512
BYTES = K * T + 16 * T + 5 * 4 * 512 * 512 + 4 * 8 * V * 4 + 5 * 128 * 32 * 2

F32 = mybir.dt.float32
BF16 = mybir.dt.bfloat16
I32 = mybir.dt.int32
U32 = mybir.dt.uint32
U16 = mybir.dt.uint16
U8 = mybir.dt.uint8
FP8X4 = mybir.dt.float8_e4m3fn_x4
MULT = mybir.AluOpType.mult
ADD = mybir.AluOpType.add
RELU = mybir.ActivationFunctionType.Relu

P = 128
PACK = 4
LANES = 16


def tile_picked_hgrid_relu_p_kernel(
    tc, x_words, x_scales, w1, a1, a2, a3, a4, w2, res, w3, offs, c1, c2, c3, c4, out
):
    nc = tc.nc
    with ExitStack() as ctx:
        lists = ctx.enter_context(tc.tile_pool(name="lists", bufs=1))
        keep = ctx.enter_context(tc.tile_pool(name="keep", bufs=1))
        psum = ctx.enter_context(tc.psum_pool(name="psum", bufs=1))

        def load_list(dram, name):
            tile = lists.tile([P, S // LANES], U16, name=name)
            nc.sync.dma_start(tile[:], dram)
            return tile

        def load_weight(dram, name):
            raw = keep.tile([P, PACK, H], F32, name=name, tag=name, align_bytes=64)
            nc.sync.dma_start(raw[:], dram.rearrange("(p j) c -> p j c", j=PACK))
            return raw

        def mx(out_ap, w_codes, w_scales, cols, codes, scales):
            nc.tensor.matmul_mx(
                out=out_ap, lhsT=w_codes[:, cols].bitcast(FP8X4), lhsT_scale=w_scales[:, cols],
                rhs=codes.bitcast(FP8X4), rhs_scale=scales, start=True, stop=True,
            )

        def quantize(codes, scales, grouped):
            nc.vector.quantize_mx(out=codes.bitcast(FP8X4), scales=scales, in_=grouped)

        w1_raw = load_weight(w1, "w1_raw")
        picked = load_list(offs, "picked")
        table_scales = keep.tile([P, T], U8, name="table_scales")
        nc.gpsimd.memset(table_scales[:].bitcast(I32), 0)
        for q in range(4):
            nc.sync.dma_start(
                table_scales[32 * q : 32 * q + 4, :].bitcast(I32),
                x_scales[0, 4 * q : 4 * q + 4, :].bitcast(I32),
            )
        table_words = keep.tile([P, T], I32, name="table_words")
        nc.sync.dma_start(table_words[:], x_words[0].rearrange("p n t -> p (n t)").bitcast(I32))

        def load_gain(dram, name):
            gain = keep.tile([P, V], F32, name=name)
            nc.sync.dma_start(gain[:], dram.rearrange("(p j) v -> p j v", j=PACK)[:, 0, :])
            return gain

        corners = [load_list(c1, "corner0")]
        gains = [load_gain(a1, "gain0")]
        corners.append(load_list(c2, "corner1"))
        gains.append(load_gain(a2, "gain1"))
        corners.append(load_list(c3, "corner2"))
        corners.append(load_list(c4, "corner3"))
        w2_raw = load_weight(w2, "w2_raw")
        gains.append(load_gain(a3, "gain2"))
        gains.append(load_gain(a4, "gain3"))
        w3_raw = load_weight(w3, "w3_raw")
        res_sb = keep.tile([P, PACK, V], F32, name="res_sb")
        nc.sync.dma_start(res_sb[:], res.rearrange("(t p) v -> p t v", p=P))

        ident = keep.tile([P, P], F32, name="ident")
        make_identity(nc, ident[:])

        def dealt_cast(copy, raw, t0, name, count=2):
            grouped = keep.tile([P, count * P * PACK], BF16, name=name, align_bytes=64)
            copy(
                out=grouped[:].rearrange("p (t m j) -> p m t j", t=count, j=PACK),
                in_=raw[:].rearrange("p j (m t) -> p m t j", t=PACK)[:, :, t0 : t0 + count, :],
            )
            return grouped

        def planes(name, width):
            codes = keep.tile([P, width], U32, name=name + "_codes", align_bytes=64)
            scales = keep.tile([P, width], U8, name=name + "_scales", align_bytes=64)
            return codes, scales

        w1_codes, w1_scales = planes("w1", H)
        w1_lo = dealt_cast(nc.vector.tensor_copy, w1_raw, 0, "w1_lo", 1)
        w1_hi = dealt_cast(nc.scalar.copy, w1_raw, 1, "w1_hi", 3)
        x_codes, x_bytes = planes("x", S)
        nc.vector.tensor_copy(x_bytes[:], table_scales[:].indirect(picked[:]))
        quantize(w1_codes[:, 0:128], w1_scales[:, 0:128], w1_lo[:])

        half = S // 2
        y = [keep.tile([P, 2 * S if t < 2 else S], F32, name="y%d" % t) for t in range(PACK)]
        for t in range(2):
            nc.vector.memset(y[t][:, S : 2 * S], 0.0)
        y0_banks = [psum.tile([P, S], F32, name="y0_bank%d" % u, tag="wide", bufs=4) for u in range(2)]
        y_banks = [psum.tile([P, S], F32, name="y_bank1", tag="wide", bufs=4),
                   psum.tile([P, S], F32, name="y_bank2", tag="last", bufs=2),
                   psum.tile([P, S], F32, name="y_bank3", tag="last", bufs=2)]
        for u in range(2):
            cols = slice(u * half, (u + 1) * half)
            nc.vector.tensor_copy(
                x_codes[:, cols],
                table_words[:].bitcast(U32).indirect(picked[:, u * half // LANES : (u + 1) * half // LANES]),
            )
            mx(y0_banks[u][:, 0:half], w1_codes, w1_scales, slice(0, P), x_codes[:, cols], x_bytes[:, cols])
        quantize(w1_codes[:, 128:256], w1_scales[:, 128:256], w1_hi[:, 0:512])
        quantize(w1_codes[:, 256:512], w1_scales[:, 256:512], w1_hi[:, 512:1536])
        for t in range(1, PACK):
            mx(y_banks[t - 1][:], w1_codes, w1_scales, slice(t * P, (t + 1) * P), x_codes[:], x_bytes[:])
        nc.scalar.copy(y[0][:, 0:half], y0_banks[0][:, 0:half])
        nc.vector.tensor_copy(y[0][:, half:S], y0_banks[1][:, 0:half])
        for t in range(1, PACK):
            nc.scalar.copy(y[t][:, 0:S], y_banks[t - 1][:])

        w2_codes, w2_scales = planes("w2", H)
        for u in range(2):
            grouped = dealt_cast(nc.scalar.copy, w2_raw, 2 * u, "w2_half%d" % u)
            quantize(w2_codes[:, 256 * u : 256 * (u + 1)], w2_scales[:, 256 * u : 256 * (u + 1)], grouped[:])
        w3_codes, w3_scales = planes("w3", N)
        w3_grouped = keep.tile([P, N, PACK], BF16, name="w3_grouped", align_bytes=64)
        nc.scalar.copy(out=w3_grouped[:], in_=w3_raw[:].rearrange("p j c -> p c j"))
        quantize(w3_codes[:], w3_scales[:], w3_grouped[:].rearrange("p c j -> p (c j)"))

        out_view = out.rearrange("(t p) v -> p t v", p=P)

        def work(shape, dtype, name, tag=None):
            return keep.tile(shape, dtype, name=name, tag=tag or name, align_bytes=64)

        def gather(term, t, c, v0, n):
            nc.vector.tensor_tensor(
                term,
                y[t][:].indirect(corners[c][:, v0 // LANES : (v0 + n) // LANES]),
                gains[c][:, v0 : v0 + n],
                MULT,
            )

        def add_turned(term, c, banks, place):
            for b, bank in enumerate(banks):
                nc.tensor.matmul(
                    bank[:, place * P : (place + 1) * P], lhsT=term[:, b * P : (b + 1) * P], rhs=ident[:],
                    is_transpose=True, start=(c == 0), stop=(c == 3),
                )

        def round_pair(pair, bank):
            nc.scalar.copy(out=pair, in_=bank[:, 0 : 2 * P].rearrange("v (e p) -> v p e", e=2))

        def turn_back(b, pairs):
            back = wide_bank("back1") if b == 1 else psum.tile([P, H], F32, name="back", tag="back", bufs=1)
            for u, pair in enumerate([low[:, b], high[b][:]][:pairs] if pairs == 2 else [low[:, b]]):
                words = pair.rearrange("v p e -> v (p e)").bitcast(F32)
                nc.tensor.transpose(back[:, u * P : (u + 1) * P], words, ident[:])
            z_grouped = work([P, P * PACK], BF16, "z_grouped%d" % b)
            nc.scalar.copy(
                out=z_grouped[:].bitcast(F32).rearrange("p (v u) -> p v u", u=2)[:, :, 0:pairs],
                in_=back[:, 0 : 2 * P].rearrange("p (u v) -> p v u", u=2)[:, :, 0:pairs],
            )
            return z_grouped

        def network(b, z_grouped, banks):
            z_codes = work([P, P], U32, "z_codes%d" % b)
            z_scales = work([P, P], U8, "z_scales%d" % b)
            quantize(z_codes[:], z_scales[:], z_grouped[:])
            hidden = psum.tile([P, H], F32, name="hidden", tag="hidden", bufs=1)
            for t in range(PACK):
                cols = slice(t * P, (t + 1) * P)
                mx(hidden[:, cols], w2_codes, w2_scales, cols, z_codes[:], z_scales[:])
            h_grouped = work([P, P * PACK], BF16, "h_grouped%d" % b)
            nc.scalar.activation(
                out=h_grouped[:].rearrange("p (v t) -> p v t", t=PACK),
                in_=hidden[:].rearrange("p (t v) -> p v t", t=PACK),
                func=RELU,
            )
            h_codes = work([P, P], U32, "h_codes%d" % b)
            h_scales = work([P, P], U8, "h_scales%d" % b)
            quantize(h_codes[:], h_scales[:], h_grouped[:])
            per_bank = PACK // len(banks)
            for t in range(PACK):
                bank = banks[t // per_bank]
                place = t % per_bank
                mx(bank[:, place * P : (place + 1) * P], w3_codes, w3_scales, slice(t * P, (t + 1) * P), h_codes[:], h_scales[:])

        def leave(queue, result, bank, t0, tiles, v0):
            nc.vector.tensor_tensor(
                result,
                bank[:, 0 : tiles * P].rearrange("p (t v) -> p t v", t=tiles),
                res_sb[:, t0 : t0 + tiles, v0 : v0 + P],
                ADD,
            )
            queue.dma_start(out_view[:, t0 : t0 + tiles, v0 : v0 + P], result)

        def wide_bank(name):
            return psum.tile([P, H], F32, name=name, tag="wide", bufs=4)

        def last_bank(b):
            return psum.tile([P, N], F32, name="last%d" % b, tag="last", bufs=2)

        low = work([P, 4, P, 2], BF16, "low", "w3_raw")
        high = [work([P, P, 2], BF16, "high%d" % b) for b in range(3)]

        sums = [wide_bank("low%d" % b) for b in range(4)]
        first = work([P, 7, V], F32, "terms_first")
        second = work([P, V + 8 * 2 * P + 7 * P], F32, "terms_second", "w2_raw")
        for t in range(2):
            for c in range(4):
                term = first[:, 4 * t + c, :] if 4 * t + c < 7 else second[:, 0:V]
                gather(term, t, c, 0, V)
                add_turned(term, c, sums, t)
        for b in range(4):
            round_pair(low[:, b], sums[b])
        z_last = turn_back(3, 1)

        sums = [wide_bank("high%d" % b) for b in range(2)]
        for e in range(2):
            for c in range(4):
                at = V + (4 * e + c) * 2 * P
                gather(second[:, at : at + 2 * P], 2 + e, c, 0, 2 * P)
                add_turned(second[:, at : at + 2 * P], c, sums, e)
        lasts = []
        for b in range(2):
            round_pair(high[b][:], sums[b])
        for b in range(2):
            lasts.append(last_bank(b))
            network(b, turn_back(b, 2), [lasts[b]])

        sums = [wide_bank("high2")]
        third = work([P, 8 - 7 + 2 * 2, P], F32, "terms_third", "high1")
        for e in range(2):
            for c in range(4):
                g = 4 * e + c
                at = V + 8 * 2 * P + g * P
                term = second[:, at : at + P] if g < 7 else third[:, g - 7, :]
                gather(term, 2 + e, c, 2 * P, P)
                add_turned(term, c, sums, e)
        round_pair(high[2][:], sums[0])
        lasts.append(wide_bank("last2"))
        network(2, turn_back(2, 2), [lasts[2]])

        v0 = 3 * P
        fourth = work([P, 2 * (3 - 2), P], F32, "terms_fourth", "z_codes0")
        fifth = work([P, 2 * (4 - 3), P], F32, "terms_fifth", "z_codes1")
        pairs = []
        for c in range(4):
            if c < 2:
                pairs.append(third[:, 8 - 7 + 2 * c : 8 - 7 + 2 * c + 2, :])
            elif c < 3:
                pairs.append(fourth[:, 2 * (c - 2) : 2 * (c - 2) + 2, :])
            else:
                pairs.append(fifth[:, 2 * (c - 3) : 2 * (c - 3) + 2, :])
            for e in range(2):
                gather(pairs[c][:, e, :], 2 + e, c, v0, P)
        partial = [work([P, 2, P], F32, "partial%d" % i) for i in range(2)]
        nc.vector.tensor_tensor(partial[0][:], pairs[0], pairs[1], ADD)
        nc.vector.tensor_tensor(partial[1][:], partial[0][:], pairs[2], ADD)
        nc.vector.tensor_tensor(
            z_last[:].rearrange("p (v t) -> p v t", t=PACK)[:, :, 2:4],
            partial[1][:].rearrange("p e v -> p v e"),
            pairs[3].rearrange("p e v -> p v e"),
            ADD,
        )
        halves = [psum.tile([P, 2 * P], F32, name="last3_%d" % u, tag="wide", bufs=4) for u in range(2)]
        network(3, z_last, halves)

        early = work([P, 2, PACK, P], F32, "early", "z_grouped3")
        for b in range(2):
            leave(nc.sync, early[:, b], lasts[b], 0, PACK, b * P)
        late = work([P, PACK, P], F32, "late", "h_grouped3")
        leave(nc.sync, late[:], lasts[2], 0, PACK, 2 * P)
        for u, queue in enumerate((nc.sync, nc.scalar)):
            result = work([P, 2, P], F32, "result%d" % u)
            leave(queue, result[:], halves[u], 2 * u, 2, v0)
